import numpy as np
import ml_dtypes


def mxq(x, axis, fmt="e4m3"):
    dtype, down = {"e4m3": (ml_dtypes.float8_e4m3fn, 7), "e5m2": (ml_dtypes.float8_e5m2, 14)}[fmt]
    v = np.moveaxis(np.asarray(x, np.float32).astype(ml_dtypes.bfloat16).astype(np.float64), axis, -1)
    blocks = v.reshape(v.shape[:-1] + (-1, 32))
    amax = np.abs(blocks).max(-1, keepdims=True)
    byte = np.maximum(np.where(amax > 0, np.frexp(amax)[1] - 1 + 127, 0) - down, 1)
    scale = np.exp2(byte - 127.0)
    codes = (blocks / scale).astype(np.float32).astype(dtype).astype(np.float64)
    return np.moveaxis((codes * scale).reshape(v.shape), -1, axis)


WIDE = False


def mx_kscale(k):
    if not WIDE:
        return np.ones(k)
    levels = np.array([10, -10, 5, -5, 0])
    if k % 512:
        return np.exp2(np.random.permutation(np.resize(levels, k // 32))).repeat(32)
    a = np.empty((k // 512, 16))
    for p in range(k // 512):
        a[p, :8] = np.random.permutation(np.resize(levels, 8))
        for g in range(8):
            far = levels[np.abs(levels - a[p, g]) >= 10]
            a[p, g + 8] = far[np.random.randint(len(far))]
    return np.exp2(a.ravel()).repeat(32)


def f64(x):
    return np.asarray(x).astype(np.float64)


def striped(idx):
    return np.tile(idx.reshape(-1, 16).T, (8, 1)).astype(np.uint16)


def unstriped(offs):
    return offs[:16].T.reshape(-1).astype(np.int64)


E2M1 = np.array([0.0, 0.5, 1.0, 1.5, 2.0, 3.0, 4.0, 6.0, -0.0, -0.5, -1.0, -1.5, -2.0, -3.0, -4.0, -6.0])


def pack_weight(w, fmt):
    k, n = w.shape
    w = f64(np.asarray(w, np.float32).astype(ml_dtypes.bfloat16)).reshape(k // 32, 32, n)
    amax = np.abs(w).max(1)
    if fmt == "e4m3":
        byte = np.frexp(amax)[1] - 1 + 127 - 7
    else:
        mant, ex = np.frexp(amax / 6.0)
        byte = np.where(mant > 0.5, ex, ex - 1) + 127
    byte = np.clip(np.where(amax > 0, byte, 1), 1, 254)
    scaled = (w * np.exp2(127.0 - byte)[:, None, :]).reshape(k, n).astype(np.float32)
    by_word = np.ascontiguousarray(scaled.reshape(k // 512, 128, 4, n).transpose(0, 1, 3, 2))
    if fmt == "e4m3":
        words = by_word.astype(ml_dtypes.float8_e4m3fn).view(np.uint8)
    else:
        c = by_word.astype(ml_dtypes.float4_e2m1fn).view(np.uint8) & 0xF
        words = (c[..., 0::2] | (c[..., 1::2] << 4)).reshape(k // 512, 128, 2 * n)
    return np.ascontiguousarray(words), np.ascontiguousarray(byte.astype(np.uint8).reshape(k // 512, 16, n))


def unpack_weight(words, scales, fmt):
    g, _, n = scales.shape
    words = np.ascontiguousarray(words).reshape(g, 128, n, -1)
    if fmt == "e4m3":
        vals = words.view(ml_dtypes.float8_e4m3fn).astype(np.float64)
    else:
        nib = np.empty((g, 128, n, 4), np.uint8)
        nib[..., 0::2] = words & 0xF
        nib[..., 1::2] = words >> 4
        vals = E2M1[nib]
    vals = vals * np.repeat(np.exp2(scales.astype(np.float64) - 127.0), 8, axis=1)[..., None]
    return vals.transpose(0, 1, 3, 2).reshape(g * 512, n)


def gelu(v):
    return 0.5 * v * (1.0 + np.tanh(np.sqrt(2.0 / np.pi) * (v + 0.044715 * v**3)))


def twice(P):
    return np.random.permutation(np.repeat(np.arange(P), 2))


K, T, S, P, H = 1536, 4096, 1024, 512, 1024

def setup_inputs():
    n = np.random.standard_normal
    s = mx_kscale(K)[:, None]
    u = mx_kscale(H)[:, None]
    d = {}
    d["tab_words"], d["tab_scales"] = pack_weight(n((K, T)) * s, "e4m3")
    d["offs"] = striped(np.random.permutation(T)[:S])
    calls = np.random.permutation(S)
    d["pos1"] = striped(calls[:P])
    d["pos2"] = striped(calls[P:2 * P])
    d["pos3"] = striped(twice(P))
    d["w1"] = (n((K, H)) / s * u.T / K ** 0.5).astype(np.float32)
    d["w2_words"], d["w2_scales"] = pack_weight(n((H, H)) / u / H ** 0.5, "e2m1")
    d["w3"] = (n((H, H)) / u / H ** 0.5).astype(np.float32)
    d["gain"] = (np.exp(0.3 * n(H)) / u[:, 0]).astype(np.float32)
    return d

def reference(tab_words, tab_scales, offs, pos1, pos2, pos3, w1, w2_words, w2_scales, w3, gain):
    v = unpack_weight(tab_words, tab_scales, "e4m3")[:, unstriped(offs)]
    w2 = unpack_weight(w2_words, w2_scales, "e2m1")
    h = mxq(f64(w1), 0, "e4m3").T @ v
    h1 = h[:, unstriped(pos1)]
    h2 = h[:, unstriped(pos2)]
    both = mxq(h1 + h2, 0, "e4m3")
    apart = mxq(np.abs(h1 - h2), 0, "e4m3")
    content = w2.T @ both
    contrast = mxq(f64(w3), 0, "e4m3").T @ apart
    y = content * np.tanh(contrast)
    raised = y[:, unstriped(pos3)]
    return np.minimum(raised, f64(gain)[:, None] * h)

@@ -1,0 +1,342 @@
+from contextlib import ExitStack
+
+import concourse.mybir as mybir
+
+K, T, S, PAIRS, H = 1536, 4096, 1024, 512, 1024
+FLOPS = 2 * K * H * S + 2 * 2 * H * H * PAIRS
+
+F32 = mybir.dt.float32
+BF16 = mybir.dt.bfloat16
+I32 = mybir.dt.int32
+U32 = mybir.dt.uint32
+U16 = mybir.dt.uint16
+U8 = mybir.dt.uint8
+FP8X4 = mybir.dt.float8_e4m3fn_x4
+FP4X4 = mybir.dt.float4_e2m1fn_x4
+ALU = mybir.AluOpType
+ACT = mybir.ActivationFunctionType
+
+P = 128
+PACK = 4
+PASS = P * PACK
+BANK = 512
+K_PASSES = K // PASS
+GROUPS = H // PASS
+
+
+def tile_list_incident_call_features_kernel(
+    tc, tab_words, tab_scales, offs, pos1, pos2, pos3, w1, w2_words, w2_scales, w3, gain, out
+):
+    nc = tc.nc
+    with ExitStack() as ctx:
+        keep = ctx.enter_context(tc.tile_pool(name="keep", bufs=1))
+        raw_pool = ctx.enter_context(tc.tile_pool(name="raw", bufs=4))
+        tanh_pool = ctx.enter_context(tc.tile_pool(name="tanh", bufs=2))
+        psum = ctx.enter_context(tc.psum_pool(name="psum", bufs=1))
+
+        def bank(i):
+            return psum.tile([P, BANK], F32, name=f"bank{i}", tag=f"bank{i}")
+
+        def slot(tag, shape, dtype, name):
+            return keep.tile(shape, dtype, name=name, tag=tag or name, align_bytes=64)
+
+        idx = keep.tile([P, S // 16], U16, name="idx")
+        p1 = keep.tile([P, PAIRS // 16], U16, name="p1")
+        p2 = keep.tile([P, PAIRS // 16], U16, name="p2")
+        p3 = keep.tile([P, S // 16], U16, name="p3")
+        gains = keep.tile([P, GROUPS, PACK], F32, name="gains")
+
+        table_scales = slot("rows", [P, T], U8, "table_scales")
+        w2_scale_rows = keep.tile([P, GROUPS, H], U8, name="w2_scale_rows", align_bytes=64)
+        nc.vector.memset(table_scales[:].bitcast(I32), 0)
+        nc.vector.memset(w2_scale_rows[:].bitcast(I32), 0)
+        for q in range(4):
+            nc.gpsimd.dma_start(
+                out=table_scales[32 * q : 32 * q + 4 * K_PASSES, :].bitcast(I32),
+                in_=tab_scales[:, 4 * q : 4 * q + 4, :].bitcast(I32),
+            )
+        for q in range(4):
+            nc.scalar.dma_start(
+                out=w2_scale_rows[32 * q : 32 * q + 4, :, :].bitcast(I32),
+                in_=w2_scales[:, 4 * q : 4 * q + 4, :].rearrange("a r c -> r a c").bitcast(I32),
+            )
+
+        def load_table(a):
+            words = slot(f"big{a}", [P, T], I32, f"table{a}")
+            nc.sync.dma_start(out=words[:], in_=tab_words[a].rearrange("p t i -> p (t i)").bitcast(I32))
+            return words
+
+        def load_weight(w, a, b, pieces=1):
+            raw = raw_pool.tile([P, PACK, PASS], F32, name="raw", tag="raw")
+            rows = w[a * PASS : (a + 1) * PASS, b * PASS : (b + 1) * PASS].rearrange("(p j) c -> p j c", j=PACK)
+            width = PASS // pieces
+            for u in range(pieces):
+                nc.sync.dma_start(out=raw[:, :, u * width : (u + 1) * width], in_=rows[:, :, u * width : (u + 1) * width])
+            return raw
+
+        def copy_on(engine, out_ap, in_ap):
+            if engine == "scalar":
+                nc.scalar.copy(out=out_ap, in_=in_ap)
+            else:
+                nc.vector.tensor_copy(out=out_ap, in_=in_ap)
+
+        def round_weight(raw, engines, tag):
+            rounded = slot(tag, [P, PACK, P, PACK], BF16, "rounded")
+            width = P // len(engines)
+            for u, engine in enumerate(engines):
+                copy_on(
+                    engine,
+                    rounded[:, :, u * width : (u + 1) * width, :].rearrange("p t m j -> p m j t"),
+                    raw[:, :, u * width * PACK : (u + 1) * width * PACK].rearrange("p j (m t) -> p m j t", t=PACK),
+                )
+            return rounded[:].rearrange("p t m j -> p (t m j)")
+
+        def planes(name, tags=(None, None)):
+            return slot(tags[0], [P, PASS], U32, name + "_codes"), slot(tags[1], [P, PASS], U8, name + "_scales")
+
+        def quantize(operand, rounded, cuts=(0, PASS)):
+            codes, scales = operand
+            for c0, c1 in zip(cuts, cuts[1:]):
+                nc.vector.quantize_mx(
+                    out=codes[:, c0:c1].bitcast(FP8X4), scales=scales[:, c0:c1], in_=rounded[:, PACK * c0 : PACK * c1]
+                )
+            return operand
+
+        nc.sync.dma_start(out=idx[:], in_=offs)
+        table, w1_raw = [], {}
+        for a in range(K_PASSES):
+            table.append(load_table(a))
+            w1_raw[a, 0] = load_weight(w1, a, 0, pieces=2 if a == K_PASSES - 1 else 1)
+        nc.sync.dma_start(out=p1[:], in_=pos1)
+        nc.sync.dma_start(out=p2[:], in_=pos2)
+        w2_raw = slot("E", [P, GROUPS, 2 * H], U8, "w2_raw")
+        nc.sync.dma_start(out=w2_raw[:].bitcast(I32), in_=w2_words.rearrange("a p c -> p a c").bitcast(I32))
+
+        picked = {}
+        h = {}
+
+        def pick_words(a, tag):
+            picked[a] = slot(tag, [P, S], U32, f"picked{a}")
+            nc.vector.tensor_copy(out=picked[a][:], in_=table[a][:].bitcast(U32).indirect(idx[:]))
+
+        def stage1_pass(banks, a, t, operand):
+            codes, scales = operand
+            for u in range(2):
+                cols = slice(u * BANK, (u + 1) * BANK)
+                nc.tensor.matmul_mx(
+                    out=banks[2 * t + u][:],
+                    lhsT=codes[:, t * P : (t + 1) * P].bitcast(FP8X4),
+                    lhsT_scale=scales[:, t * P : (t + 1) * P],
+                    rhs=picked[a][:, cols].bitcast(FP8X4),
+                    rhs_scale=picked_scales[4 * a :, cols],
+                    start=(a == 0),
+                    stop=(a == K_PASSES - 1),
+                )
+
+        def empty_h(banks, b, t, tag=None):
+            h[b, t] = slot(tag, [P, S], F32, f"h{b}{t}")
+            for u in range(2):
+                nc.scalar.copy(out=h[b, t][:, u * BANK : (u + 1) * BANK], in_=banks[2 * t + u][:])
+
+        last_cuts = (0, P, 2 * P, PASS)
+        banks = [bank(i) for i in range(8)]
+        pick_words(0, "D")
+        picked_scales = slot("big0", [P, S], U8, "picked_scales")
+        nc.vector.tensor_copy(out=picked_scales[:], in_=table_scales[:].indirect(idx[:]))
+        w2_sc = slot("rows", [P, GROUPS * H], U8, "w2_sc")
+        nc.vector.tensor_copy(
+            out=w2_sc[:].rearrange("p (g t c i) -> p g c t i", t=PACK, c=8, i=16),
+            in_=w2_scale_rows[:].rearrange("p a n -> p (a n)").rearrange("p (g c i t) -> p g c t i", t=PACK, c=8, i=16),
+        )
+        for a, tag in enumerate("ABC"):
+            last = a == K_PASSES - 1
+            rounded = round_weight(w1_raw[a, 0], ("scalar", "vector") if last else ("scalar",), tag)
+            operand = planes(f"w1_{a}0", ("F", "G") if last else (None, None))
+            quantize(operand, rounded, last_cuts if last else (0, PASS))
+            for t in range(PACK):
+                stage1_pass(banks, a, t, operand)
+            if not last:
+                pick_words(a + 1, tag)
+
+        for a in range(K_PASSES):
+            w1_raw[a, 1] = load_weight(w1, a, 1)
+        nc.sync.dma_start(out=p3[:], in_=pos3)
+        nc.sync.dma_start(out=gains[:], in_=gain.rearrange("(b p t) -> p b t", p=P, t=PACK))
+        w3_raw = {(a, b): load_weight(w3, a, b) for b in range(GROUPS) for a in range(GROUPS)}
+
+        w2_codes = slot("C", [P, GROUPS * 2 * H], U8, "w2_codes")
+        nc.vector.tensor_copy(
+            out=w2_codes[:].bitcast(U16).rearrange("p (g t c i) -> p g c t i", t=PACK, c=16, i=8),
+            in_=w2_raw[:].rearrange("p a n -> p (a n)").bitcast(U16).rearrange("p (g c i t) -> p g c t i", t=PACK, c=16, i=8),
+        )
+
+        def pair_tiles(name, width, tags):
+            return slot(tags[0], [P, PACK, width], F32, name + "_sums"), slot(tags[1], [P, PACK, width], F32, name + "_diffs")
+
+        def pair_up(tiles, b, t, m0, m1):
+            sums, diffs = tiles
+            lists = slice(m0 // 16, m1 // 16)
+            nc.vector.tensor_copy(out=sums[:, t, :], in_=h[b, t][:].indirect(p1[:, lists]))
+            nc.vector.tensor_tensor(diffs[:, t, :], h[b, t][:].indirect(p2[:, lists]), sums[:, t, :], ALU.subtract)
+
+        def add_up(tiles, t):
+            sums, diffs = tiles
+            nc.vector.scalar_tensor_tensor(sums[:, t, :], sums[:, t, :], 2.0, diffs[:, t, :], ALU.mult, ALU.add)
+
+        def weave(dst, src, m0, m1, func):
+            nc.scalar.activation(
+                dst[:, m0:m1, :].rearrange("p (c i) t -> p c t i", i=4),
+                src[:].rearrange("p t (c i) -> p c t i", i=4),
+                func,
+            )
+
+        first_banks = banks
+        banks = {}
+        pairs0 = pair_tiles("pairs0", PAIRS, ("sums", "diffs"))
+        empty_h(first_banks, 0, 0)
+        empty_h(first_banks, 0, 1)
+        w1_q = {}
+        pair_up(pairs0, 0, 0, 0, PAIRS)
+        w1_q[0] = quantize(planes("w1_01"), round_weight(w1_raw[0, 1], ("vector",), "E"))
+        add_up(pairs0, 0)
+        pair_up(pairs0, 0, 1, 0, PAIRS)
+        w1_q[1] = quantize(planes("w1_11"), round_weight(w1_raw[1, 1], ("scalar",), "F"))
+        add_up(pairs0, 1)
+        empty_h(first_banks, 0, 2, "F")
+        w1_q[2] = quantize(planes("w1_21"), round_weight(w1_raw[2, 1], ("scalar",), "G"))
+        empty_h(first_banks, 0, 3, "G")
+        for t in range(PACK):
+            banks[2 * t], banks[2 * t + 1] = bank(2 * t), bank(2 * t + 1)
+            for a in range(K_PASSES):
+                stage1_pass(banks, a, t, w1_q[a])
+        for t in (2, 3):
+            pair_up(pairs0, 0, t, 0, PAIRS)
+            add_up(pairs0, t)
+        for t in range(PACK):
+            empty_h(banks, 1, t)
+
+        both, apart, w3_q = {}, {}, {}
+
+        def woven(name, tag):
+            return slot(tag, [P, PAIRS, PACK], BF16, name)
+
+        def flat(tile):
+            return tile[:].rearrange("p m t -> p (m t)")
+
+        def contrast_pass(banks, b, t, a):
+            cols = slice(t * P, (t + 1) * P)
+            nc.tensor.matmul_mx(
+                out=banks[2 * t + 1][:],
+                lhsT=w3_q[a, b][0][:, cols].bitcast(FP8X4),
+                lhsT_scale=w3_q[a, b][1][:, cols],
+                rhs=apart[a][0][:].bitcast(FP8X4),
+                rhs_scale=apart[a][1][:],
+                start=(a == 0),
+                stop=(a == GROUPS - 1),
+            )
+
+        def content_pass(banks, b, t, a):
+            g = (a * GROUPS + b) * PASS + t * P
+            nc.tensor.matmul_mx(
+                out=banks[2 * t][:],
+                lhsT=w2_codes[:, 2 * g : 2 * (g + P)].bitcast(FP4X4),
+                lhsT_scale=w2_sc[:, g : g + P],
+                rhs=both[a][0][:].bitcast(FP8X4),
+                rhs_scale=both[a][1][:],
+                start=(a == 0),
+                stop=(a == GROUPS - 1),
+            )
+
+        def stage2_pass(banks, b, t, a):
+            contrast_pass(banks, b, t, a)
+            content_pass(banks, b, t, a)
+
+        half = PAIRS // 2
+        both_woven, apart_woven = woven("both0", "B"), woven("apart0", "A")
+        weave(both_woven, pairs0[0], 0, PAIRS, ACT.Copy)
+        weave(apart_woven, pairs0[1], 0, PAIRS, ACT.Abs)
+        pairs1 = pair_tiles("pairs1a", half, (None, None))
+        for t in range(PACK):
+            pair_up(pairs1, 1, t, 0, half)
+            if t > 0:
+                add_up(pairs1, t - 1)
+        both[0] = quantize(planes("both0"), flat(both_woven))
+        add_up(pairs1, PACK - 1)
+        apart[0] = quantize(planes("apart0"), flat(apart_woven))
+        both_woven, apart_woven = woven("both1", "D"), woven("apart1", "E")
+        both[1], apart[1] = planes("both1"), planes("apart1")
+        weave(apart_woven, pairs1[1], 0, half, ACT.Abs)
+        weave(both_woven, pairs1[0], 0, half, ACT.Copy)
+        rounded = round_weight(w3_raw[0, 0], ("scalar",), "B")
+        banks = [bank(i) for i in range(8)]
+        for t in range(PACK):
+            content_pass(banks, 0, t, 0)
+        pairs1 = pair_tiles("pairs1b", half, ("sums", "diffs"))
+        for t in range(PACK):
+            pair_up(pairs1, 1, t, half, PAIRS)
+            if t > 0:
+                add_up(pairs1, t - 1)
+            if t == 1:
+                quantize(apart[1], flat(apart_woven), (0, half))
+            if t == 2:
+                quantize(both[1], flat(both_woven), (0, half))
+        add_up(pairs1, PACK - 1)
+        w3_q[0, 0] = quantize(planes("w3_00"), rounded)
+        for t in range(PACK):
+            contrast_pass(banks, 0, t, 0)
+        weave(apart_woven, pairs1[1], half, PAIRS, ACT.Abs)
+        weave(both_woven, pairs1[0], half, PAIRS, ACT.Copy)
+        w3_q[1, 0] = quantize(planes("w3_10"), round_weight(w3_raw[1, 0], ("vector",), "A"))
+        quantize(apart[1], flat(apart_woven), (half, PAIRS))
+        quantize(both[1], flat(both_woven), (half, PAIRS))
+
+        y = slot("big1", [P, GROUPS * PACK * PAIRS], F32, "y")
+        staged = [slot(tag, [P, PACK, S], F32, "staged_" + tag) for tag in ("big2", "big0")]
+        out_rows = out.rearrange("(b p t) j -> b t p j", p=P, t=PACK)
+        slices = [(b, t) for b in range(GROUPS) for t in range(PACK)]
+
+        def y_start(s):
+            return (len(slices) - 1 - s) * PAIRS
+
+        def make_y(banks, s):
+            b, t = slices[s]
+            th = tanh_pool.tile([P, PAIRS], F32, name="th", tag="th")
+            nc.scalar.activation(th[:], banks[2 * t + 1][:], ACT.Tanh)
+            nc.vector.tensor_tensor(y[:, y_start(s) : y_start(s) + PAIRS], banks[2 * t][:], th[:], ALU.mult)
+
+        def raise_y(s, j0, j1):
+            b, t = slices[s]
+            width = min(s + 1, 3) * PAIRS
+            piece = min({1: 256, 2: 512, 3: 1024}[min(s + 1, 3)], j1 - j0)
+            window = y[:, y_start(s) : y_start(s) + width]
+            for j in range(j0, j1, piece):
+                nc.vector.tensor_copy(out=staged[b][:, t, j : j + piece], in_=window.indirect(p3[:, j // 16 : (j + piece) // 16]))
+
+        def finish(s, j0, j1):
+            b, t = slices[s]
+            rows = staged[b][:, t, j0:j1]
+            nc.vector.scalar_tensor_tensor(rows, h[b, t][:, j0:j1], gains[:, b, t : t + 1], rows, ALU.mult, ALU.min)
+            nc.sync.dma_start(out=out_rows[b, t][:, j0:j1], in_=rows)
+
+        for t in range(PACK):
+            stage2_pass(banks, 0, t, 1)
+        later_banks = {}
+        make_y(banks, 0)
+        for s in range(len(slices)):
+            b, t = slices[s]
+            if s + 1 < len(slices):
+                raise_y(s, 0, S)
+                make_y(banks if s + 1 < PACK else later_banks, s + 1)
+                finish(s, 0, S)
+                if s < GROUPS:
+                    w3_q[s, 1] = quantize(planes(f"w3_{s}1"), round_weight(w3_raw[s, 1], ("scalar",), "ED"[s]))
+                if s in (1, 2):
+                    for t2 in ((0, 1, 2) if s == 1 else (3,)):
+                        later_banks[2 * t2], later_banks[2 * t2 + 1] = bank(2 * t2), bank(2 * t2 + 1)
+                        for a in range(GROUPS):
+                            stage2_pass(later_banks, 1, t2, a)
+            else:
+                raise_y(s, 0, S // 2)
+                raise_y(s, S // 2, S)
+                finish(s, 0, S // 2)
+                finish(s, S // 2, S)

@@ -30,7 +30,7 @@ def tile_list_incident_call_features_kernel(
     nc = tc.nc
     with ExitStack() as ctx:
         keep = ctx.enter_context(tc.tile_pool(name="keep", bufs=1))
-        raw_pool = ctx.enter_context(tc.tile_pool(name="raw", bufs=4))
+        raw_pool = ctx.enter_context(tc.tile_pool(name="raw", bufs=3))
         tanh_pool = ctx.enter_context(tc.tile_pool(name="tanh", bufs=2))
         psum = ctx.enter_context(tc.psum_pool(name="psum", bufs=1))
 
@@ -52,11 +52,6 @@ def tile_list_incident_call_features_kernel(
         nc.vector.memset(w2_scale_rows[:].bitcast(I32), 0)
         for q in range(4):
             nc.gpsimd.dma_start(
-                out=table_scales[32 * q : 32 * q + 4 * K_PASSES, :].bitcast(I32),
-                in_=tab_scales[:, 4 * q : 4 * q + 4, :].bitcast(I32),
-            )
-        for q in range(4):
-            nc.scalar.dma_start(
                 out=w2_scale_rows[32 * q : 32 * q + 4, :, :].bitcast(I32),
                 in_=w2_scales[:, 4 * q : 4 * q + 4, :].rearrange("a r c -> r a c").bitcast(I32),
             )
@@ -66,8 +61,11 @@ def tile_list_incident_call_features_kernel(
             nc.sync.dma_start(out=words[:], in_=tab_words[a].rearrange("p t i -> p (t i)").bitcast(I32))
             return words
 
-        def load_weight(w, a, b, pieces=1):
-            raw = raw_pool.tile([P, PACK, PASS], F32, name="raw", tag="raw")
+        def load_weight(w, a, b, pieces=1, tag=None):
+            if tag is None:
+                raw = raw_pool.tile([P, PACK, PASS], F32, name="raw", tag="raw")
+            else:
+                raw = slot(tag, [P, PACK, PASS], F32, tag)
             rows = w[a * PASS : (a + 1) * PASS, b * PASS : (b + 1) * PASS].rearrange("(p j) c -> p j c", j=PACK)
             width = PASS // pieces
             for u in range(pieces):
@@ -106,7 +104,13 @@ def tile_list_incident_call_features_kernel(
         table, w1_raw = [], {}
         for a in range(K_PASSES):
             table.append(load_table(a))
-            w1_raw[a, 0] = load_weight(w1, a, 0, pieces=2 if a == K_PASSES - 1 else 1)
+            if a == 0:
+                for q in range(4):
+                    nc.sync.dma_start(
+                        out=table_scales[32 * q : 32 * q + 4 * K_PASSES, :].bitcast(I32),
+                        in_=tab_scales[:, 4 * q : 4 * q + 4, :].bitcast(I32),
+                    )
+            w1_raw[a, 0] = load_weight(w1, a, 0, 2, "raw_last") if a == K_PASSES - 1 else load_weight(w1, a, 0)
         nc.sync.dma_start(out=p1[:], in_=pos1)
         nc.sync.dma_start(out=p2[:], in_=pos2)
         w2_raw = slot("E", [P, GROUPS, 2 * H], U8, "w2_raw")
@@ -143,11 +147,6 @@ def tile_list_incident_call_features_kernel(
         pick_words(0, "D")
         picked_scales = slot("big0", [P, S], U8, "picked_scales")
         nc.vector.tensor_copy(out=picked_scales[:], in_=table_scales[:].indirect(idx[:]))
-        w2_sc = slot("rows", [P, GROUPS * H], U8, "w2_sc")
-        nc.vector.tensor_copy(
-            out=w2_sc[:].rearrange("p (g t c i) -> p g c t i", t=PACK, c=8, i=16),
-            in_=w2_scale_rows[:].rearrange("p a n -> p (a n)").rearrange("p (g c i t) -> p g c t i", t=PACK, c=8, i=16),
-        )
         for a, tag in enumerate("ABC"):
             last = a == K_PASSES - 1
             rounded = round_weight(w1_raw[a, 0], ("scalar", "vector") if last else ("scalar",), tag)
@@ -159,7 +158,7 @@ def tile_list_incident_call_features_kernel(
                 pick_words(a + 1, tag)
 
         for a in range(K_PASSES):
-            w1_raw[a, 1] = load_weight(w1, a, 1)
+            w1_raw[a, 1] = load_weight(w1, a, 1, 1, (None, "raw_h2", "raw_h3")[a])
         nc.sync.dma_start(out=p3[:], in_=pos3)
         nc.sync.dma_start(out=gains[:], in_=gain.rearrange("(b p t) -> p b t", p=P, t=PACK))
         w3_raw = {(a, b): load_weight(w3, a, b) for b in range(GROUPS) for a in range(GROUPS)}
@@ -169,19 +168,37 @@ def tile_list_incident_call_features_kernel(
             out=w2_codes[:].bitcast(U16).rearrange("p (g t c i) -> p g c t i", t=PACK, c=16, i=8),
             in_=w2_raw[:].rearrange("p a n -> p (a n)").bitcast(U16).rearrange("p (g c i t) -> p g c t i", t=PACK, c=16, i=8),
         )
+        w2_sc = slot("raw_last", [P, GROUPS * H], U8, "w2_sc")
+        nc.vector.tensor_copy(
+            out=w2_sc[:].rearrange("p (g t c i) -> p g c t i", t=PACK, c=8, i=16),
+            in_=w2_scale_rows[:].rearrange("p a n -> p (a n)").rearrange("p (g c i t) -> p g c t i", t=PACK, c=8, i=16),
+        )
 
         def pair_tiles(name, width, tags):
             return slot(tags[0], [P, PACK, width], F32, name + "_sums"), slot(tags[1], [P, PACK, width], F32, name + "_diffs")
 
-        def pair_up(tiles, b, t, m0, m1):
-            sums, diffs = tiles
-            lists = slice(m0 // 16, m1 // 16)
-            nc.vector.tensor_copy(out=sums[:, t, :], in_=h[b, t][:].indirect(p1[:, lists]))
-            nc.vector.tensor_tensor(diffs[:, t, :], h[b, t][:].indirect(p2[:, lists]), sums[:, t, :], ALU.subtract)
+        def pick_first(tiles, b, t, m0, c0, c1):
+            lists = slice((m0 + c0) // 16, (m0 + c1) // 16)
+            nc.vector.tensor_copy(out=tiles[0][:, t, c0:c1], in_=h[b, t][:].indirect(p1[:, lists]))
 
-        def add_up(tiles, t):
-            sums, diffs = tiles
-            nc.vector.scalar_tensor_tensor(sums[:, t, :], sums[:, t, :], 2.0, diffs[:, t, :], ALU.mult, ALU.add)
+        def pick_second(tiles, b, t, m0, c0, c1):
+            lists = slice((m0 + c0) // 16, (m0 + c1) // 16)
+            nc.vector.tensor_tensor(
+                tiles[1][:, t, c0:c1], h[b, t][:].indirect(p2[:, lists]), tiles[0][:, t, c0:c1], ALU.subtract
+            )
+
+        def add_up(tiles, t, c0, c1):
+            sums, diffs = tiles[0][:, t, c0:c1], tiles[1][:, t, c0:c1]
+            nc.vector.scalar_tensor_tensor(sums, sums, 2.0, diffs, ALU.mult, ALU.add)
+
+        def pair_up(tiles, b, t, m0, width):
+            pieces = [(0, width // 2), (width // 2, width)]
+            for c0, c1 in pieces:
+                pick_first(tiles, b, t, m0, c0, c1)
+            for c0, c1 in pieces:
+                pick_second(tiles, b, t, m0, c0, c1)
+            for c0, c1 in pieces:
+                add_up(tiles, t, c0, c1)
 
         def weave(dst, src, m0, m1, func):
             nc.scalar.activation(
@@ -197,25 +214,22 @@ def tile_list_incident_call_features_kernel(
         empty_h(first_banks, 0, 1)
         w1_q = {}
         pair_up(pairs0, 0, 0, 0, PAIRS)
-        w1_q[0] = quantize(planes("w1_01"), round_weight(w1_raw[0, 1], ("vector",), "E"))
-        add_up(pairs0, 0)
+        w1_q[0] = quantize(planes("w1_01"), round_weight(w1_raw[0, 1], ("scalar",), "E"))
         pair_up(pairs0, 0, 1, 0, PAIRS)
         w1_q[1] = quantize(planes("w1_11"), round_weight(w1_raw[1, 1], ("scalar",), "F"))
-        add_up(pairs0, 1)
-        empty_h(first_banks, 0, 2, "F")
+        empty_h(first_banks, 0, 2, "raw_h2")
         w1_q[2] = quantize(planes("w1_21"), round_weight(w1_raw[2, 1], ("scalar",), "G"))
-        empty_h(first_banks, 0, 3, "G")
+        empty_h(first_banks, 0, 3, "raw_h3")
         for t in range(PACK):
             banks[2 * t], banks[2 * t + 1] = bank(2 * t), bank(2 * t + 1)
             for a in range(K_PASSES):
                 stage1_pass(banks, a, t, w1_q[a])
         for t in (2, 3):
             pair_up(pairs0, 0, t, 0, PAIRS)
-            add_up(pairs0, t)
+        both, apart, w3_q, w3_rounded = {}, {}, {}, {}
+        w3_rounded[0, 0] = round_weight(w3_raw[0, 0], ("scalar",), "F")
         for t in range(PACK):
             empty_h(banks, 1, t)
-
-        both, apart, w3_q = {}, {}, {}
 
         def woven(name, tag):
             return slot(tag, [P, PAIRS, PACK], BF16, name)
@@ -255,38 +269,39 @@ def tile_list_incident_call_features_kernel(
         both_woven, apart_woven = woven("both0", "B"), woven("apart0", "A")
         weave(both_woven, pairs0[0], 0, PAIRS, ACT.Copy)
         weave(apart_woven, pairs0[1], 0, PAIRS, ACT.Abs)
+        w3_rounded[1, 0] = round_weight(w3_raw[1, 0], ("scalar",), "big0")
         pairs1 = pair_tiles("pairs1a", half, (None, None))
         for t in range(PACK):
             pair_up(pairs1, 1, t, 0, half)
-            if t > 0:
-                add_up(pairs1, t - 1)
         both[0] = quantize(planes("both0"), flat(both_woven))
-        add_up(pairs1, PACK - 1)
         apart[0] = quantize(planes("apart0"), flat(apart_woven))
+        w3_q[0, 0] = quantize(planes("w3_00"), w3_rounded[0, 0])
         both_woven, apart_woven = woven("both1", "D"), woven("apart1", "E")
         both[1], apart[1] = planes("both1"), planes("apart1")
         weave(apart_woven, pairs1[1], 0, half, ACT.Abs)
         weave(both_woven, pairs1[0], 0, half, ACT.Copy)
-        rounded = round_weight(w3_raw[0, 0], ("scalar",), "B")
+        w3_rounded[0, 1] = round_weight(w3_raw[0, 1], ("scalar",), "B")
+        w3_rounded[1, 1] = round_weight(w3_raw[1, 1], ("scalar",), "A")
         banks = [bank(i) for i in range(8)]
         for t in range(PACK):
-            content_pass(banks, 0, t, 0)
+            stage2_pass(banks, 0, t, 0)
         pairs1 = pair_tiles("pairs1b", half, ("sums", "diffs"))
         for t in range(PACK):
-            pair_up(pairs1, 1, t, half, PAIRS)
+            pick_first(pairs1, 1, t, half, 0, half)
             if t > 0:
-                add_up(pairs1, t - 1)
+                add_up(pairs1, t - 1, 0, half)
+            pick_second(pairs1, 1, t, half, 0, half)
+            if t == 0:
+                w3_q[1, 0] = quantize(planes("w3_10"), w3_rounded[1, 0])
             if t == 1:
                 quantize(apart[1], flat(apart_woven), (0, half))
             if t == 2:
                 quantize(both[1], flat(both_woven), (0, half))
-        add_up(pairs1, PACK - 1)
-        w3_q[0, 0] = quantize(planes("w3_00"), rounded)
-        for t in range(PACK):
-            contrast_pass(banks, 0, t, 0)
+        add_up(pairs1, PACK - 1, 0, half)
         weave(apart_woven, pairs1[1], half, PAIRS, ACT.Abs)
         weave(both_woven, pairs1[0], half, PAIRS, ACT.Copy)
-        w3_q[1, 0] = quantize(planes("w3_10"), round_weight(w3_raw[1, 0], ("vector",), "A"))
+        for a in range(GROUPS):
+            w3_q[a, 1] = quantize(planes(f"w3_{a}1"), w3_rounded[a, 1])
         quantize(apart[1], flat(apart_woven), (half, PAIRS))
         quantize(both[1], flat(both_woven), (half, PAIRS))
 
@@ -328,8 +343,6 @@ def tile_list_incident_call_features_kernel(
                 raise_y(s, 0, S)
                 make_y(banks if s + 1 < PACK else later_banks, s + 1)
                 finish(s, 0, S)
-                if s < GROUPS:
-                    w3_q[s, 1] = quantize(planes(f"w3_{s}1"), round_weight(w3_raw[s, 1], ("scalar",), "ED"[s]))
                 if s in (1, 2):
                     for t2 in ((0, 1, 2) if s == 1 else (3,)):
                         later_banks[2 * t2], later_banks[2 * t2 + 1] = bank(2 * t2), bank(2 * t2 + 1)

@@ -1,6 +1,7 @@
 from contextlib import ExitStack
 
 import concourse.mybir as mybir
+from concourse.masks import make_identity
 
 K, T, S, PAIRS, H = 1536, 4096, 1024, 512, 1024
 FLOPS = 2 * K * H * S + 2 * 2 * H * H * PAIRS
@@ -22,6 +23,7 @@ PASS = P * PACK
 BANK = 512
 K_PASSES = K // PASS
 GROUPS = H // PASS
+SCALAR_SHARE = 44
 
 
 def tile_list_incident_call_features_kernel(
@@ -31,7 +33,8 @@ def tile_list_incident_call_features_kernel(
     with ExitStack() as ctx:
         keep = ctx.enter_context(tc.tile_pool(name="keep", bufs=1))
         raw_pool = ctx.enter_context(tc.tile_pool(name="raw", bufs=3))
-        tanh_pool = ctx.enter_context(tc.tile_pool(name="tanh", bufs=2))
+        tanh_pool = ctx.enter_context(tc.tile_pool(name="tanh", bufs=3))
+        turn_pool = ctx.enter_context(tc.tile_pool(name="turn", bufs=4))
         psum = ctx.enter_context(tc.psum_pool(name="psum", bufs=1))
 
         def bank(i):
@@ -46,10 +49,18 @@ def tile_list_incident_call_features_kernel(
         p3 = keep.tile([P, S // 16], U16, name="p3")
         gains = keep.tile([P, GROUPS, PACK], F32, name="gains")
 
+        identity = keep.tile([P, P], F32, name="identity")
+        make_identity(nc, identity[:])
+
         table_scales = slot("rows", [P, T], U8, "table_scales")
         w2_scale_rows = keep.tile([P, GROUPS, H], U8, name="w2_scale_rows", align_bytes=64)
         nc.vector.memset(table_scales[:].bitcast(I32), 0)
         nc.vector.memset(w2_scale_rows[:].bitcast(I32), 0)
+        for q in range(4):
+            nc.gpsimd.dma_start(
+                out=table_scales[32 * q : 32 * q + 4 * K_PASSES, :].bitcast(I32),
+                in_=tab_scales[:, 4 * q : 4 * q + 4, :].bitcast(I32),
+            )
         for q in range(4):
             nc.gpsimd.dma_start(
                 out=w2_scale_rows[32 * q : 32 * q + 4, :, :].bitcast(I32),
@@ -80,12 +91,12 @@ def tile_list_incident_call_features_kernel(
 
         def round_weight(raw, engines, tag):
             rounded = slot(tag, [P, PACK, P, PACK], BF16, "rounded")
-            width = P // len(engines)
-            for u, engine in enumerate(engines):
+            cuts = (0, P) if len(engines) == 1 else (0, SCALAR_SHARE, P)
+            for m0, m1, engine in zip(cuts, cuts[1:], engines):
                 copy_on(
                     engine,
-                    rounded[:, :, u * width : (u + 1) * width, :].rearrange("p t m j -> p m j t"),
-                    raw[:, :, u * width * PACK : (u + 1) * width * PACK].rearrange("p j (m t) -> p m j t", t=PACK),
+                    rounded[:, :, m0:m1, :].rearrange("p t m j -> p m j t"),
+                    raw[:, :, m0 * PACK : m1 * PACK].rearrange("p j (m t) -> p m j t", t=PACK),
                 )
             return rounded[:].rearrange("p t m j -> p (t m j)")
 
@@ -104,20 +115,14 @@ def tile_list_incident_call_features_kernel(
         table, w1_raw = [], {}
         for a in range(K_PASSES):
             table.append(load_table(a))
-            if a == 0:
-                for q in range(4):
-                    nc.sync.dma_start(
-                        out=table_scales[32 * q : 32 * q + 4 * K_PASSES, :].bitcast(I32),
-                        in_=tab_scales[:, 4 * q : 4 * q + 4, :].bitcast(I32),
-                    )
-            w1_raw[a, 0] = load_weight(w1, a, 0, 2, "raw_last") if a == K_PASSES - 1 else load_weight(w1, a, 0)
+            w1_raw[a, 0] = load_weight(w1, a, 0, 1, "raw_last") if a == K_PASSES - 1 else load_weight(w1, a, 0)
         nc.sync.dma_start(out=p1[:], in_=pos1)
         nc.sync.dma_start(out=p2[:], in_=pos2)
         w2_raw = slot("E", [P, GROUPS, 2 * H], U8, "w2_raw")
         nc.sync.dma_start(out=w2_raw[:].bitcast(I32), in_=w2_words.rearrange("a p c -> p a c").bitcast(I32))
 
         picked = {}
-        h = {}
+        h, h_tag = {}, {}
 
         def pick_words(a, tag):
             picked[a] = slot(tag, [P, S], U32, f"picked{a}")
@@ -138,6 +143,7 @@ def tile_list_incident_call_features_kernel(
                 )
 
         def empty_h(banks, b, t, tag=None):
+            h_tag[b, t] = tag or f"h{b}{t}"
             h[b, t] = slot(tag, [P, S], F32, f"h{b}{t}")
             for u in range(2):
                 nc.scalar.copy(out=h[b, t][:, u * BANK : (u + 1) * BANK], in_=banks[2 * t + u][:])
@@ -197,8 +203,35 @@ def tile_list_incident_call_features_kernel(
                 pick_first(tiles, b, t, m0, c0, c1)
             for c0, c1 in pieces:
                 pick_second(tiles, b, t, m0, c0, c1)
-            for c0, c1 in pieces:
-                add_up(tiles, t, c0, c1)
+
+        def turn(out_ap, in_ap, start, stop):
+            nc.tensor.matmul(out_ap, in_ap, identity[:], start=start, stop=stop, is_transpose=True)
+
+        def add_turned(tiles, sum_banks, t):
+            for k, sum_bank in enumerate(sum_banks):
+                cols = slice(k * P, (k + 1) * P)
+                terms = (tiles[0], tiles[0], tiles[1])
+                for n, term in enumerate(terms):
+                    turn(sum_bank[:, t * P : (t + 1) * P], term[:, t, cols], n == 0, n == len(terms) - 1)
+
+        def weave_turned(dst, m0, sum_banks, word_bank_numbers):
+            turned = []
+            for sum_bank in sum_banks:
+                rows = turn_pool.tile([P, 2, P, 2], BF16, name="turned", tag="turned")
+                nc.scalar.copy(out=rows[:], in_=sum_bank[:].rearrange("m (u e p) -> m u p e", u=2, e=2))
+                turned.append(rows)
+            for i, number in enumerate(word_bank_numbers):
+                word_bank = bank(number)
+                for k in range(2):
+                    words = turned[2 * i + k][:].rearrange("m u p e -> m (u p e)").bitcast(F32)
+                    for u in range(2):
+                        c = (2 * k + u) * P
+                        turn(word_bank[:, c : c + P], words[:, u * P : (u + 1) * P], True, True)
+                m = m0 + 2 * P * i
+                nc.scalar.copy(
+                    out=dst[:, m : m + 2 * P, :].rearrange("p m t -> p (m t)").bitcast(F32).rearrange("p (k m u) -> p k m u", k=2, u=2),
+                    in_=word_bank[:].rearrange("p (k u m) -> p k m u", k=2, u=2),
+                )
 
         def weave(dst, src, m0, m1, func):
             nc.scalar.activation(
@@ -213,8 +246,9 @@ def tile_list_incident_call_features_kernel(
         empty_h(first_banks, 0, 0)
         empty_h(first_banks, 0, 1)
         w1_q = {}
+        rounded = round_weight(w1_raw[0, 1], ("vector",), "E")
         pair_up(pairs0, 0, 0, 0, PAIRS)
-        w1_q[0] = quantize(planes("w1_01"), round_weight(w1_raw[0, 1], ("scalar",), "E"))
+        w1_q[0] = quantize(planes("w1_01"), rounded)
         pair_up(pairs0, 0, 1, 0, PAIRS)
         w1_q[1] = quantize(planes("w1_11"), round_weight(w1_raw[1, 1], ("scalar",), "F"))
         empty_h(first_banks, 0, 2, "raw_h2")
@@ -267,32 +301,32 @@ def tile_list_incident_call_features_kernel(
 
         half = PAIRS // 2
         both_woven, apart_woven = woven("both0", "B"), woven("apart0", "A")
-        weave(both_woven, pairs0[0], 0, PAIRS, ACT.Copy)
+        sum_banks = [bank(i) for i in range(4)]
+        for t in range(PACK):
+            add_turned(pairs0, sum_banks, t)
+        weave_turned(both_woven, 0, sum_banks, (4, 5))
         weave(apart_woven, pairs0[1], 0, PAIRS, ACT.Abs)
-        w3_rounded[1, 0] = round_weight(w3_raw[1, 0], ("scalar",), "big0")
         pairs1 = pair_tiles("pairs1a", half, (None, None))
+        sum_banks = [bank(6), bank(7)]
         for t in range(PACK):
             pair_up(pairs1, 1, t, 0, half)
+            add_turned(pairs1, sum_banks, t)
         both[0] = quantize(planes("both0"), flat(both_woven))
         apart[0] = quantize(planes("apart0"), flat(apart_woven))
         w3_q[0, 0] = quantize(planes("w3_00"), w3_rounded[0, 0])
         both_woven, apart_woven = woven("both1", "D"), woven("apart1", "E")
         both[1], apart[1] = planes("both1"), planes("apart1")
         weave(apart_woven, pairs1[1], 0, half, ACT.Abs)
-        weave(both_woven, pairs1[0], 0, half, ACT.Copy)
-        w3_rounded[0, 1] = round_weight(w3_raw[0, 1], ("scalar",), "B")
-        w3_rounded[1, 1] = round_weight(w3_raw[1, 1], ("scalar",), "A")
+        weave_turned(both_woven, 0, sum_banks, (4,))
         banks = [bank(i) for i in range(8)]
         for t in range(PACK):
             stage2_pass(banks, 0, t, 0)
-        pairs1 = pair_tiles("pairs1b", half, ("sums", "diffs"))
+        pairs1 = pair_tiles("pairs1b", half, ("sums", None))
         for t in range(PACK):
             pick_first(pairs1, 1, t, half, 0, half)
             if t > 0:
                 add_up(pairs1, t - 1, 0, half)
             pick_second(pairs1, 1, t, half, 0, half)
-            if t == 0:
-                w3_q[1, 0] = quantize(planes("w3_10"), w3_rounded[1, 0])
             if t == 1:
                 quantize(apart[1], flat(apart_woven), (0, half))
             if t == 2:
@@ -300,8 +334,7 @@ def tile_list_incident_call_features_kernel(
         add_up(pairs1, PACK - 1, 0, half)
         weave(apart_woven, pairs1[1], half, PAIRS, ACT.Abs)
         weave(both_woven, pairs1[0], half, PAIRS, ACT.Copy)
-        for a in range(GROUPS):
-            w3_q[a, 1] = quantize(planes(f"w3_{a}1"), w3_rounded[a, 1])
+        w3_q[1, 0] = quantize(planes("w3_10"), round_weight(w3_raw[1, 0], ("vector",), "A"))
         quantize(apart[1], flat(apart_woven), (half, PAIRS))
         quantize(both[1], flat(both_woven), (half, PAIRS))
 
@@ -317,39 +350,47 @@ def tile_list_incident_call_features_kernel(
             b, t = slices[s]
             th = tanh_pool.tile([P, PAIRS], F32, name="th", tag="th")
             nc.scalar.activation(th[:], banks[2 * t + 1][:], ACT.Tanh)
-            nc.vector.tensor_tensor(y[:, y_start(s) : y_start(s) + PAIRS], banks[2 * t][:], th[:], ALU.mult)
+            y_cols = y[:, y_start(s) : y_start(s) + PAIRS]
+            if s == 0:
+                nc.vector.tensor_tensor(y_cols, banks[2 * t][:], th[:], ALU.mult)
+            else:
+                content = slot(h_tag[slices[s - 2]] if s >= 2 else None, [P, PAIRS], F32, "content")
+                nc.scalar.copy(out=content[:], in_=banks[2 * t][:])
+                nc.gpsimd.tensor_tensor(y_cols, content[:], th[:], ALU.mult)
 
-        def raise_y(s, j0, j1):
+        def raise_y(s):
             b, t = slices[s]
-            width = min(s + 1, 3) * PAIRS
-            piece = min({1: 256, 2: 512, 3: 1024}[min(s + 1, 3)], j1 - j0)
+            width = min(s + 1, 2) * PAIRS
+            piece = width // 2
             window = y[:, y_start(s) : y_start(s) + width]
-            for j in range(j0, j1, piece):
+            for j in range(0, S, piece):
                 nc.vector.tensor_copy(out=staged[b][:, t, j : j + piece], in_=window.indirect(p3[:, j // 16 : (j + piece) // 16]))
 
-        def finish(s, j0, j1):
+        def finish(s):
             b, t = slices[s]
-            rows = staged[b][:, t, j0:j1]
-            nc.vector.scalar_tensor_tensor(rows, h[b, t][:, j0:j1], gains[:, b, t : t + 1], rows, ALU.mult, ALU.min)
-            nc.sync.dma_start(out=out_rows[b, t][:, j0:j1], in_=rows)
+            for j0 in (0, S // 2):
+                cols = slice(j0, j0 + S // 2)
+                rows = staged[b][:, t, cols]
+                nc.vector.scalar_tensor_tensor(rows, h[b, t][:, cols], gains[:, b, t : t + 1], rows, ALU.mult, ALU.min)
+                if s + 1 == len(slices):
+                    nc.sync.dma_start(out=out_rows[b, t][:, cols], in_=rows)
+            if s + 1 < len(slices):
+                nc.sync.dma_start(out=out_rows[b, t], in_=staged[b][:, t, :])
 
         for t in range(PACK):
             stage2_pass(banks, 0, t, 1)
         later_banks = {}
         make_y(banks, 0)
+        make_y(banks, 1)
         for s in range(len(slices)):
-            b, t = slices[s]
-            if s + 1 < len(slices):
-                raise_y(s, 0, S)
-                make_y(banks if s + 1 < PACK else later_banks, s + 1)
-                finish(s, 0, S)
-                if s in (1, 2):
-                    for t2 in ((0, 1, 2) if s == 1 else (3,)):
-                        later_banks[2 * t2], later_banks[2 * t2 + 1] = bank(2 * t2), bank(2 * t2 + 1)
-                        for a in range(GROUPS):
-                            stage2_pass(later_banks, 1, t2, a)
-            else:
-                raise_y(s, 0, S // 2)
-                raise_y(s, S // 2, S)
-                finish(s, 0, S // 2)
-                finish(s, S // 2, S)
+            raise_y(s)
+            finish(s)
+            if s + 2 < len(slices):
+                make_y(banks if s + 2 < PACK else later_banks, s + 2)
+            if s < GROUPS:
+                w3_q[s, 1] = quantize(planes(f"w3_{s}1"), round_weight(w3_raw[s, 1], ("scalar",), "ED"[s]))
+            if s == 1:
+                for t in range(PACK):
+                    later_banks[2 * t], later_banks[2 * t + 1] = bank(2 * t), bank(2 * t + 1)
+                    for a in range(GROUPS):
+                        stage2_pass(later_banks, 1, t, a)

from contextlib import ExitStack

import concourse.mybir as mybir
from concourse.masks import make_identity

K, T, S, PAIRS, H = 1536, 4096, 1024, 512, 1024
FLOPS = 2 * K * H * S + 2 * 2 * H * H * PAIRS

F32 = mybir.dt.float32
BF16 = mybir.dt.bfloat16
I32 = mybir.dt.int32
U32 = mybir.dt.uint32
U16 = mybir.dt.uint16
U8 = mybir.dt.uint8
FP8X4 = mybir.dt.float8_e4m3fn_x4
FP4X4 = mybir.dt.float4_e2m1fn_x4
ALU = mybir.AluOpType
ACT = mybir.ActivationFunctionType

P = 128
PACK = 4
PASS = P * PACK
BANK = 512
K_PASSES = K // PASS
GROUPS = H // PASS
SCALAR_SHARE = 44


def tile_list_incident_call_features_kernel(
    tc, tab_words, tab_scales, offs, pos1, pos2, pos3, w1, w2_words, w2_scales, w3, gain, out
):
    nc = tc.nc
    with ExitStack() as ctx:
        keep = ctx.enter_context(tc.tile_pool(name="keep", bufs=1))
        raw_pool = ctx.enter_context(tc.tile_pool(name="raw", bufs=3))
        tanh_pool = ctx.enter_context(tc.tile_pool(name="tanh", bufs=3))
        turn_pool = ctx.enter_context(tc.tile_pool(name="turn", bufs=4))
        psum = ctx.enter_context(tc.psum_pool(name="psum", bufs=1))

        def bank(i):
            return psum.tile([P, BANK], F32, name=f"bank{i}", tag=f"bank{i}")

        def slot(tag, shape, dtype, name):
            return keep.tile(shape, dtype, name=name, tag=tag or name, align_bytes=64)

        idx = keep.tile([P, S // 16], U16, name="idx")
        p1 = keep.tile([P, PAIRS // 16], U16, name="p1")
        p2 = keep.tile([P, PAIRS // 16], U16, name="p2")
        p3 = keep.tile([P, S // 16], U16, name="p3")
        gains = keep.tile([P, GROUPS, PACK], F32, name="gains")

        identity = keep.tile([P, P], F32, name="identity")
        make_identity(nc, identity[:])

        table_scales = slot("rows", [P, T], U8, "table_scales")
        w2_scale_rows = keep.tile([P, GROUPS, H], U8, name="w2_scale_rows", align_bytes=64)
        nc.vector.memset(table_scales[:].bitcast(I32), 0)
        nc.vector.memset(w2_scale_rows[:].bitcast(I32), 0)
        for q in range(4):
            nc.gpsimd.dma_start(
                out=table_scales[32 * q : 32 * q + 4 * K_PASSES, :].bitcast(I32),
                in_=tab_scales[:, 4 * q : 4 * q + 4, :].bitcast(I32),
            )
        for q in range(4):
            nc.gpsimd.dma_start(
                out=w2_scale_rows[32 * q : 32 * q + 4, :, :].bitcast(I32),
                in_=w2_scales[:, 4 * q : 4 * q + 4, :].rearrange("a r c -> r a c").bitcast(I32),
            )

        def load_table(a):
            words = slot(f"big{a}", [P, T], I32, f"table{a}")
            nc.sync.dma_start(out=words[:], in_=tab_words[a].rearrange("p t i -> p (t i)").bitcast(I32))
            return words

        def load_weight(w, a, b, pieces=1, tag=None):
            if tag is None:
                raw = raw_pool.tile([P, PACK, PASS], F32, name="raw", tag="raw")
            else:
                raw = slot(tag, [P, PACK, PASS], F32, tag)
            rows = w[a * PASS : (a + 1) * PASS, b * PASS : (b + 1) * PASS].rearrange("(p j) c -> p j c", j=PACK)
            width = PASS // pieces
            for u in range(pieces):
                nc.sync.dma_start(out=raw[:, :, u * width : (u + 1) * width], in_=rows[:, :, u * width : (u + 1) * width])
            return raw

        def copy_on(engine, out_ap, in_ap):
            if engine == "scalar":
                nc.scalar.copy(out=out_ap, in_=in_ap)
            else:
                nc.vector.tensor_copy(out=out_ap, in_=in_ap)

        def round_weight(raw, engines, tag):
            rounded = slot(tag, [P, PACK, P, PACK], BF16, "rounded")
            cuts = (0, P) if len(engines) == 1 else (0, SCALAR_SHARE, P)
            for m0, m1, engine in zip(cuts, cuts[1:], engines):
                copy_on(
                    engine,
                    rounded[:, :, m0:m1, :].rearrange("p t m j -> p m j t"),
                    raw[:, :, m0 * PACK : m1 * PACK].rearrange("p j (m t) -> p m j t", t=PACK),
                )
            return rounded[:].rearrange("p t m j -> p (t m j)")

        def planes(name, tags=(None, None)):
            return slot(tags[0], [P, PASS], U32, name + "_codes"), slot(tags[1], [P, PASS], U8, name + "_scales")

        def quantize(operand, rounded, cuts=(0, PASS)):
            codes, scales = operand
            for c0, c1 in zip(cuts, cuts[1:]):
                nc.vector.quantize_mx(
                    out=codes[:, c0:c1].bitcast(FP8X4), scales=scales[:, c0:c1], in_=rounded[:, PACK * c0 : PACK * c1]
                )
            return operand

        nc.sync.dma_start(out=idx[:], in_=offs)
        table, w1_raw = [], {}
        for a in range(K_PASSES):
            table.append(load_table(a))
            w1_raw[a, 0] = load_weight(w1, a, 0, 1, "raw_last") if a == K_PASSES - 1 else load_weight(w1, a, 0)
        nc.sync.dma_start(out=p1[:], in_=pos1)
        nc.sync.dma_start(out=p2[:], in_=pos2)
        w2_raw = slot("E", [P, GROUPS, 2 * H], U8, "w2_raw")
        nc.sync.dma_start(out=w2_raw[:].bitcast(I32), in_=w2_words.rearrange("a p c -> p a c").bitcast(I32))

        picked = {}
        h, h_tag = {}, {}

        def pick_words(a, tag):
            picked[a] = slot(tag, [P, S], U32, f"picked{a}")
            nc.vector.tensor_copy(out=picked[a][:], in_=table[a][:].bitcast(U32).indirect(idx[:]))

        def stage1_pass(banks, a, t, operand):
            codes, scales = operand
            for u in range(2):
                cols = slice(u * BANK, (u + 1) * BANK)
                nc.tensor.matmul_mx(
                    out=banks[2 * t + u][:],
                    lhsT=codes[:, t * P : (t + 1) * P].bitcast(FP8X4),
                    lhsT_scale=scales[:, t * P : (t + 1) * P],
                    rhs=picked[a][:, cols].bitcast(FP8X4),
                    rhs_scale=picked_scales[4 * a :, cols],
                    start=(a == 0),
                    stop=(a == K_PASSES - 1),
                )

        def empty_h(banks, b, t, tag=None):
            h_tag[b, t] = tag or f"h{b}{t}"
            h[b, t] = slot(tag, [P, S], F32, f"h{b}{t}")
            for u in range(2):
                nc.scalar.copy(out=h[b, t][:, u * BANK : (u + 1) * BANK], in_=banks[2 * t + u][:])

        last_cuts = (0, P, 2 * P, PASS)
        banks = [bank(i) for i in range(8)]
        pick_words(0, "D")
        picked_scales = slot("big0", [P, S], U8, "picked_scales")
        nc.vector.tensor_copy(out=picked_scales[:], in_=table_scales[:].indirect(idx[:]))
        for a, tag in enumerate("ABC"):
            last = a == K_PASSES - 1
            rounded = round_weight(w1_raw[a, 0], ("scalar", "vector") if last else ("scalar",), tag)
            operand = planes(f"w1_{a}0", ("F", "G") if last else (None, None))
            quantize(operand, rounded, last_cuts if last else (0, PASS))
            for t in range(PACK):
                stage1_pass(banks, a, t, operand)
            if not last:
                pick_words(a + 1, tag)

        for a in range(K_PASSES):
            w1_raw[a, 1] = load_weight(w1, a, 1, 1, (None, "raw_h2", "raw_h3")[a])
        nc.sync.dma_start(out=p3[:], in_=pos3)
        nc.sync.dma_start(out=gains[:], in_=gain.rearrange("(b p t) -> p b t", p=P, t=PACK))
        w3_raw = {(a, b): load_weight(w3, a, b) for b in range(GROUPS) for a in range(GROUPS)}

        w2_codes = slot("C", [P, GROUPS * 2 * H], U8, "w2_codes")
        nc.vector.tensor_copy(
            out=w2_codes[:].bitcast(U16).rearrange("p (g t c i) -> p g c t i", t=PACK, c=16, i=8),
            in_=w2_raw[:].rearrange("p a n -> p (a n)").bitcast(U16).rearrange("p (g c i t) -> p g c t i", t=PACK, c=16, i=8),
        )
        w2_sc = slot("raw_last", [P, GROUPS * H], U8, "w2_sc")
        nc.vector.tensor_copy(
            out=w2_sc[:].rearrange("p (g t c i) -> p g c t i", t=PACK, c=8, i=16),
            in_=w2_scale_rows[:].rearrange("p a n -> p (a n)").rearrange("p (g c i t) -> p g c t i", t=PACK, c=8, i=16),
        )

        def pair_tiles(name, width, tags):
            return slot(tags[0], [P, PACK, width], F32, name + "_sums"), slot(tags[1], [P, PACK, width], F32, name + "_diffs")

        def pick_first(tiles, b, t, m0, c0, c1):
            lists = slice((m0 + c0) // 16, (m0 + c1) // 16)
            nc.vector.tensor_copy(out=tiles[0][:, t, c0:c1], in_=h[b, t][:].indirect(p1[:, lists]))

        def pick_second(tiles, b, t, m0, c0, c1):
            lists = slice((m0 + c0) // 16, (m0 + c1) // 16)
            nc.vector.tensor_tensor(
                tiles[1][:, t, c0:c1], h[b, t][:].indirect(p2[:, lists]), tiles[0][:, t, c0:c1], ALU.subtract
            )

        def add_up(tiles, t, c0, c1):
            sums, diffs = tiles[0][:, t, c0:c1], tiles[1][:, t, c0:c1]
            nc.vector.scalar_tensor_tensor(sums, sums, 2.0, diffs, ALU.mult, ALU.add)

        def pair_up(tiles, b, t, m0, width):
            pieces = [(0, width // 2), (width // 2, width)]
            for c0, c1 in pieces:
                pick_first(tiles, b, t, m0, c0, c1)
            for c0, c1 in pieces:
                pick_second(tiles, b, t, m0, c0, c1)

        def turn(out_ap, in_ap, start, stop):
            nc.tensor.matmul(out_ap, in_ap, identity[:], start=start, stop=stop, is_transpose=True)

        def add_turned(tiles, sum_banks, t):
            for k, sum_bank in enumerate(sum_banks):
                cols = slice(k * P, (k + 1) * P)
                terms = (tiles[0], tiles[0], tiles[1])
                for n, term in enumerate(terms):
                    turn(sum_bank[:, t * P : (t + 1) * P], term[:, t, cols], n == 0, n == len(terms) - 1)

        def weave_turned(dst, m0, sum_banks, word_bank_numbers):
            turned = []
            for sum_bank in sum_banks:
                rows = turn_pool.tile([P, 2, P, 2], BF16, name="turned", tag="turned")
                nc.scalar.copy(out=rows[:], in_=sum_bank[:].rearrange("m (u e p) -> m u p e", u=2, e=2))
                turned.append(rows)
            for i, number in enumerate(word_bank_numbers):
                word_bank = bank(number)
                for k in range(2):
                    words = turned[2 * i + k][:].rearrange("m u p e -> m (u p e)").bitcast(F32)
                    for u in range(2):
                        c = (2 * k + u) * P
                        turn(word_bank[:, c : c + P], words[:, u * P : (u + 1) * P], True, True)
                m = m0 + 2 * P * i
                nc.scalar.copy(
                    out=dst[:, m : m + 2 * P, :].rearrange("p m t -> p (m t)").bitcast(F32).rearrange("p (k m u) -> p k m u", k=2, u=2),
                    in_=word_bank[:].rearrange("p (k u m) -> p k m u", k=2, u=2),
                )

        def weave(dst, src, m0, m1, func):
            nc.scalar.activation(
                dst[:, m0:m1, :].rearrange("p (c i) t -> p c t i", i=4),
                src[:].rearrange("p t (c i) -> p c t i", i=4),
                func,
            )

        first_banks = banks
        banks = {}
        pairs0 = pair_tiles("pairs0", PAIRS, ("sums", "diffs"))
        empty_h(first_banks, 0, 0)
        empty_h(first_banks, 0, 1)
        w1_q = {}
        rounded = round_weight(w1_raw[0, 1], ("vector",), "E")
        pair_up(pairs0, 0, 0, 0, PAIRS)
        w1_q[0] = quantize(planes("w1_01"), rounded)
        pair_up(pairs0, 0, 1, 0, PAIRS)
        w1_q[1] = quantize(planes("w1_11"), round_weight(w1_raw[1, 1], ("scalar",), "F"))
        empty_h(first_banks, 0, 2, "raw_h2")
        w1_q[2] = quantize(planes("w1_21"), round_weight(w1_raw[2, 1], ("scalar",), "G"))
        empty_h(first_banks, 0, 3, "raw_h3")
        for t in range(PACK):
            banks[2 * t], banks[2 * t + 1] = bank(2 * t), bank(2 * t + 1)
            for a in range(K_PASSES):
                stage1_pass(banks, a, t, w1_q[a])
        for t in (2, 3):
            pair_up(pairs0, 0, t, 0, PAIRS)
        both, apart, w3_q, w3_rounded = {}, {}, {}, {}
        w3_rounded[0, 0] = round_weight(w3_raw[0, 0], ("scalar",), "F")
        for t in range(PACK):
            empty_h(banks, 1, t)

        def woven(name, tag):
            return slot(tag, [P, PAIRS, PACK], BF16, name)

        def flat(tile):
            return tile[:].rearrange("p m t -> p (m t)")

        def contrast_pass(banks, b, t, a):
            cols = slice(t * P, (t + 1) * P)
            nc.tensor.matmul_mx(
                out=banks[2 * t + 1][:],
                lhsT=w3_q[a, b][0][:, cols].bitcast(FP8X4),
                lhsT_scale=w3_q[a, b][1][:, cols],
                rhs=apart[a][0][:].bitcast(FP8X4),
                rhs_scale=apart[a][1][:],
                start=(a == 0),
                stop=(a == GROUPS - 1),
            )

        def content_pass(banks, b, t, a):
            g = (a * GROUPS + b) * PASS + t * P
            nc.tensor.matmul_mx(
                out=banks[2 * t][:],
                lhsT=w2_codes[:, 2 * g : 2 * (g + P)].bitcast(FP4X4),
                lhsT_scale=w2_sc[:, g : g + P],
                rhs=both[a][0][:].bitcast(FP8X4),
                rhs_scale=both[a][1][:],
                start=(a == 0),
                stop=(a == GROUPS - 1),
            )

        def stage2_pass(banks, b, t, a):
            contrast_pass(banks, b, t, a)
            content_pass(banks, b, t, a)

        half = PAIRS // 2
        both_woven, apart_woven = woven("both0", "B"), woven("apart0", "A")
        sum_banks = [bank(i) for i in range(4)]
        for t in range(PACK):
            add_turned(pairs0, sum_banks, t)
        weave_turned(both_woven, 0, sum_banks, (4, 5))
        weave(apart_woven, pairs0[1], 0, PAIRS, ACT.Abs)
        pairs1 = pair_tiles("pairs1a", half, (None, None))
        sum_banks = [bank(6), bank(7)]
        for t in range(PACK):
            pair_up(pairs1, 1, t, 0, half)
            add_turned(pairs1, sum_banks, t)
        both[0] = quantize(planes("both0"), flat(both_woven))
        apart[0] = quantize(planes("apart0"), flat(apart_woven))
        w3_q[0, 0] = quantize(planes("w3_00"), w3_rounded[0, 0])
        both_woven, apart_woven = woven("both1", "D"), woven("apart1", "E")
        both[1], apart[1] = planes("both1"), planes("apart1")
        weave(apart_woven, pairs1[1], 0, half, ACT.Abs)
        weave_turned(both_woven, 0, sum_banks, (4,))
        banks = [bank(i) for i in range(8)]
        for t in range(PACK):
            stage2_pass(banks, 0, t, 0)
        pairs1 = pair_tiles("pairs1b", half, ("sums", None))
        for t in range(PACK):
            pick_first(pairs1, 1, t, half, 0, half)
            if t > 0:
                add_up(pairs1, t - 1, 0, half)
            pick_second(pairs1, 1, t, half, 0, half)
            if t == 1:
                quantize(apart[1], flat(apart_woven), (0, half))
            if t == 2:
                quantize(both[1], flat(both_woven), (0, half))
        add_up(pairs1, PACK - 1, 0, half)
        weave(apart_woven, pairs1[1], half, PAIRS, ACT.Abs)
        weave(both_woven, pairs1[0], half, PAIRS, ACT.Copy)
        w3_q[1, 0] = quantize(planes("w3_10"), round_weight(w3_raw[1, 0], ("vector",), "A"))
        quantize(apart[1], flat(apart_woven), (half, PAIRS))
        quantize(both[1], flat(both_woven), (half, PAIRS))

        y = slot("big1", [P, GROUPS * PACK * PAIRS], F32, "y")
        staged = [slot(tag, [P, PACK, S], F32, "staged_" + tag) for tag in ("big2", "big0")]
        out_rows = out.rearrange("(b p t) j -> b t p j", p=P, t=PACK)
        slices = [(b, t) for b in range(GROUPS) for t in range(PACK)]

        def y_start(s):
            return (len(slices) - 1 - s) * PAIRS

        def make_y(banks, s):
            b, t = slices[s]
            th = tanh_pool.tile([P, PAIRS], F32, name="th", tag="th")
            nc.scalar.activation(th[:], banks[2 * t + 1][:], ACT.Tanh)
            y_cols = y[:, y_start(s) : y_start(s) + PAIRS]
            if s == 0:
                nc.vector.tensor_tensor(y_cols, banks[2 * t][:], th[:], ALU.mult)
            else:
                content = slot(h_tag[slices[s - 2]] if s >= 2 else None, [P, PAIRS], F32, "content")
                nc.scalar.copy(out=content[:], in_=banks[2 * t][:])
                nc.gpsimd.tensor_tensor(y_cols, content[:], th[:], ALU.mult)

        def raise_y(s):
            b, t = slices[s]
            width = min(s + 1, 2) * PAIRS
            piece = width // 2
            window = y[:, y_start(s) : y_start(s) + width]
            for j in range(0, S, piece):
                nc.vector.tensor_copy(out=staged[b][:, t, j : j + piece], in_=window.indirect(p3[:, j // 16 : (j + piece) // 16]))

        def finish(s):
            b, t = slices[s]
            for j0 in (0, S // 2):
                cols = slice(j0, j0 + S // 2)
                rows = staged[b][:, t, cols]
                nc.vector.scalar_tensor_tensor(rows, h[b, t][:, cols], gains[:, b, t : t + 1], rows, ALU.mult, ALU.min)
                if s + 1 == len(slices):
                    nc.sync.dma_start(out=out_rows[b, t][:, cols], in_=rows)
            if s + 1 < len(slices):
                nc.sync.dma_start(out=out_rows[b, t], in_=staged[b][:, t, :])

        for t in range(PACK):
            stage2_pass(banks, 0, t, 1)
        later_banks = {}
        make_y(banks, 0)
        make_y(banks, 1)
        for s in range(len(slices)):
            raise_y(s)
            finish(s)
            if s + 2 < len(slices):
                make_y(banks if s + 2 < PACK else later_banks, s + 2)
            if s < GROUPS:
                w3_q[s, 1] = quantize(planes(f"w3_{s}1"), round_weight(w3_raw[s, 1], ("scalar",), "ED"[s]))
            if s == 1:
                for t in range(PACK):
                    later_banks[2 * t], later_banks[2 * t + 1] = bank(2 * t), bank(2 * t + 1)
                    for a in range(GROUPS):
                        stage2_pass(later_banks, 1, t, a)
